import numpy as np
import ml_dtypes


def mxq(x, axis, fmt="e4m3"):
    dtype, down = {"e4m3": (ml_dtypes.float8_e4m3fn, 7), "e5m2": (ml_dtypes.float8_e5m2, 14)}[fmt]
    v = np.moveaxis(np.asarray(x, np.float32).astype(ml_dtypes.bfloat16).astype(np.float64), axis, -1)
    blocks = v.reshape(v.shape[:-1] + (-1, 32))
    amax = np.abs(blocks).max(-1, keepdims=True)
    byte = np.maximum(np.where(amax > 0, np.frexp(amax)[1] - 1 + 127, 0) - down, 1)
    scale = np.exp2(byte - 127.0)
    codes = (blocks / scale).astype(np.float32).astype(dtype).astype(np.float64)
    return np.moveaxis((codes * scale).reshape(v.shape), -1, axis)


WIDE = False


def mx_kscale(k):
    if not WIDE:
        return np.ones(k)
    levels = np.array([30, -30])
    if k % 512:
        return np.exp2(np.random.permutation(np.resize(levels, k // 32))).repeat(32)
    a = np.empty((k // 512, 16))
    for p in range(k // 512):
        a[p, :8] = np.random.permutation(np.resize(levels, 8))
        for g in range(8):
            far = levels[np.abs(levels - a[p, g]) >= 10]
            a[p, g + 8] = far[np.random.randint(len(far))]
    return np.exp2(a.ravel()).repeat(32)


def f64(x):
    return np.asarray(x).astype(np.float64)


def striped(idx):
    return np.tile(np.asarray(idx).reshape(-1, 16).T, (8, 1)).astype(np.uint16)


def unstriped(offs):
    return offs[:16].T.reshape(-1).astype(np.int64)


E2M1 = np.array([0.0, 0.5, 1.0, 1.5, 2.0, 3.0, 4.0, 6.0, -0.0, -0.5, -1.0, -1.5, -2.0, -3.0, -4.0, -6.0])


def pack_weight(w, fmt):
    k, n = w.shape
    w = f64(np.asarray(w, np.float32).astype(ml_dtypes.bfloat16)).reshape(k // 32, 32, n)
    amax = np.abs(w).max(1)
    if fmt in ("e4m3", "e5m2"):
        byte = np.frexp(amax)[1] - 1 + 127 - (7 if fmt == "e4m3" else 14)
    else:
        mant, ex = np.frexp(amax / 6.0)
        byte = np.where(mant > 0.5, ex, ex - 1) + 127
    byte = np.clip(np.where(amax > 0, byte, 1), 1, 254)
    scaled = (w * np.exp2(127.0 - byte)[:, None, :]).reshape(k, n).astype(np.float32)
    by_word = np.ascontiguousarray(scaled.reshape(k // 512, 128, 4, n).transpose(0, 1, 3, 2))
    if fmt in ("e4m3", "e5m2"):
        words = by_word.astype(ml_dtypes.float8_e4m3fn if fmt == "e4m3" else ml_dtypes.float8_e5m2).view(np.uint8)
    else:
        c = by_word.astype(ml_dtypes.float4_e2m1fn).view(np.uint8) & 0xF
        words = (c[..., 0::2] | (c[..., 1::2] << 4)).reshape(k // 512, 128, 2 * n)
    return np.ascontiguousarray(words), np.ascontiguousarray(byte.astype(np.uint8).reshape(k // 512, 16, n))


def unpack_weight(words, scales, fmt):
    g, _, n = scales.shape
    words = np.ascontiguousarray(words).reshape(g, 128, n, -1)
    if fmt in ("e4m3", "e5m2"):
        vals = words.view(ml_dtypes.float8_e4m3fn if fmt == "e4m3" else ml_dtypes.float8_e5m2).astype(np.float64)
    else:
        nib = np.empty((g, 128, n, 4), np.uint8)
        nib[..., 0::2] = words & 0xF
        nib[..., 1::2] = words >> 4
        vals = E2M1[nib]
    vals = vals * np.repeat(np.exp2(scales.astype(np.float64) - 127.0), 8, axis=1)[..., None]
    return vals.transpose(0, 1, 3, 2).reshape(g * 512, n)


K, T, Z, J, R, C, O, N, E = 512, 1024, 1024, 256, 512, 512, 256, 256, 128


def setup_inputs():
    n = np.random.standard_normal
    idx = np.random.permutation(T)[:J]
    idx2 = np.random.permutation(Z)[:J]
    idx3 = np.random.permutation(C)[:J]
    idx4 = np.random.permutation(C)[:J]
    idx5 = np.random.permutation(C)[:O]
    idx6 = np.random.permutation(O)[:E]
    idx7 = np.random.permutation(O)[:E]
    fk = mx_kscale(K)
    fr = mx_kscale(R)
    xtp = pack_weight(n((K, T)) / fk[:, None], "e5m2")
    xop = pack_weight(n((K, Z)) / fk[:, None], "e4m3")
    wp = pack_weight(n((K, R)) * 1 / np.sqrt(K) * fk[:, None] * fr, "e2m1")
    w2p = pack_weight(n((K, R)) * 1 / np.sqrt(K) * fk[:, None] * fr, "e5m2")
    wbp = pack_weight(n((R, N)) * 1 / np.sqrt(R) / fr[:, None], "e2m1")
    return {
        "xt_words": xtp[0],
        "xt_scales": xtp[1],
        "xo_words": xop[0],
        "xo_scales": xop[1],
        "w_words": wp[0],
        "w_scales": wp[1],
        "w2_words": w2p[0],
        "w2_scales": w2p[1],
        "wb_words": wbp[0],
        "wb_scales": wbp[1],
        "offs": striped(idx),
        "offs2": striped(idx2),
        "offs3": striped(idx3),
        "offs4": striped(idx4),
        "offs5": striped(idx5),
        "offs6": striped(idx6),
        "offs7": striped(idx7),
    }


def reference(xt_words, xt_scales, xo_words, xo_scales, w_words, w_scales, w2_words, w2_scales, wb_words, wb_scales, offs, offs2, offs3, offs4, offs5, offs6, offs7):
    idx = unstriped(offs)
    idx2 = unstriped(offs2)
    idx3 = unstriped(offs3)
    idx4 = unstriped(offs4)
    idx5 = unstriped(offs5)
    idx6 = unstriped(offs6)
    idx7 = unstriped(offs7)
    xtu = unpack_weight(xt_words, xt_scales, "e5m2")
    xou = unpack_weight(xo_words, xo_scales, "e4m3")
    wu = unpack_weight(w_words, w_scales, "e2m1")
    w2u = unpack_weight(w2_words, w2_scales, "e5m2")
    wbu = unpack_weight(wb_words, wb_scales, "e2m1")
    xtidxg = xtu[:, idx]
    xoidx2g = xou[:, idx2]
    a = wu.T @ xtidxg + w2u.T @ xoidx2g
    b = w2u.T @ xtidxg + wu.T @ xoidx2g
    pw = np.zeros((R, C))
    pw[:, idx3] = a
    pv = np.zeros((R, C))
    pv[:, idx4] = b
    pg = pw + pv
    hid = pg[:, idx5]
    hidq = mxq(hid, 0, "e4m3")
    p = wbu.T @ hidq
    y = np.maximum(p[:, idx6], p[:, idx7])
    return y

@@ -1,0 +1,170 @@
+from contextlib import ExitStack
+
+import concourse.mybir as mybir
+
+K, T, Z, J, R, C, O, N, E = 512, 1024, 1024, 256, 512, 512, 256, 256, 128
+FLOPS = 2 * (4 * K * R * J + R * N * O)
+
+F32 = mybir.dt.float32
+BF16 = mybir.dt.bfloat16
+I32 = mybir.dt.int32
+U32 = mybir.dt.uint32
+U16 = mybir.dt.uint16
+U8 = mybir.dt.uint8
+E4M3 = mybir.dt.float8_e4m3fn_x4
+E5M2 = mybir.dt.float8_e5m2_x4
+E2M1 = mybir.dt.float4_e2m1fn_x4
+COPY = mybir.ActivationFunctionType.Copy
+ADD = mybir.AluOpType.add
+MAX = mybir.AluOpType.max
+
+P = 128
+PACK = 4
+
+
+def tile_list_crossed_shared_one_bestoftwo_kernel(
+    tc, xt_words, xt_scales, xo_words, xo_scales, w_words, w_scales, w2_words, w2_scales,
+    wb_words, wb_scales, offs, offs2, offs3, offs4, offs5, offs6, offs7, out,
+):
+    nc = tc.nc
+    with ExitStack() as ctx:
+        sb = ctx.enter_context(tc.tile_pool(name="sb", bufs=1))
+        psum = ctx.enter_context(tc.psum_pool(name="psum", bufs=1))
+
+        def load_list(src, name):
+            tile = sb.tile(list(src.shape), U16, name=name)
+            nc.sync.dma_start(tile[:], src)
+            return tile
+
+        def load_words(src, width_bytes, name):
+            tile = sb.tile([P, width_bytes // 4], U32, name=name, align_bytes=64)
+            nc.sync.dma_start(tile[:].bitcast(I32), src.bitcast(I32))
+            return tile
+
+        def zero_plane(width, name):
+            tile = sb.tile([P, width], U8, name=name, align_bytes=64)
+            nc.vector.memset(tile[:].bitcast(I32), 0)
+            return tile
+
+        def load_scales(queue, tile, src):
+            for row in range(4):
+                queue.dma_start(tile[row:P:32, :].bitcast(I32), src[0, row:16:4, :].bitcast(I32))
+
+        xt_plane = zero_plane(T, "xt_plane")
+        xo_plane = zero_plane(Z, "xo_plane")
+        w2_plane = zero_plane(R, "w2_plane")
+        w_plane = zero_plane(R, "w_plane")
+        wb_plane = zero_plane(N, "wb_plane")
+
+        xt_all = load_words(xt_words[0].rearrange("p n t -> p (n t)"), 4 * T, "xt_all")
+        xo_all = load_words(xo_words[0].rearrange("p n t -> p (n t)"), 4 * Z, "xo_all")
+        idx = load_list(offs, "idx")
+        idx2 = load_list(offs2, "idx2")
+        load_scales(nc.scalar, xt_plane, xt_scales)
+        w2_raw = load_words(w2_words[0].rearrange("p n t -> p (n t)"), 4 * R, "w2_raw")
+        w_raw = load_words(w_words[0], 2 * R, "w_raw")
+        load_scales(nc.scalar, xo_plane, xo_scales)
+        load_scales(nc.scalar, w2_plane, w2_scales)
+        load_scales(nc.scalar, w_plane, w_scales)
+        idx3 = load_list(offs3, "idx3")
+        idx4 = load_list(offs4, "idx4")
+        idx5 = load_list(offs5, "idx5")
+        wb_raw = load_words(wb_words[0], 2 * N, "wb_raw")
+        load_scales(nc.sync, wb_plane, wb_scales)
+        idx6 = load_list(offs6, "idx6")
+        idx7 = load_list(offs7, "idx7")
+
+        xt_codes = sb.tile([P, J], U32, align_bytes=64)
+        xt_sc = sb.tile([P, J], U8, align_bytes=64)
+        xo_codes = sb.tile([P, J], U32, align_bytes=64)
+        xo_sc = sb.tile([P, J], U8, align_bytes=64)
+        nc.vector.tensor_copy(xt_sc[:], xt_plane[:].indirect(idx[:]))
+        nc.vector.tensor_copy(xt_codes[:], xt_all[:].indirect(idx[:]))
+        nc.vector.tensor_copy(xo_sc[:], xo_plane[:].indirect(idx2[:]))
+        nc.vector.tensor_copy(xo_codes[:], xo_all[:].indirect(idx2[:]))
+
+        w2_codes = sb.tile([P, PACK, P], U32, align_bytes=64)
+        w_codes = sb.tile([P, PACK, P], U16, align_bytes=64)
+        w2_sc = sb.tile([P, PACK, P], U8, align_bytes=64)
+        w_sc = sb.tile([P, PACK, P], U8, align_bytes=64)
+        nc.scalar.copy(w2_codes[:], w2_raw[:].rearrange("p (m t) -> p t m", t=PACK))
+        nc.vector.tensor_copy(w2_sc[:], w2_plane[:].rearrange("p (m t) -> p t m", t=PACK))
+        nc.scalar.copy(w_codes[:], w_raw[:].bitcast(U16).rearrange("p (m t) -> p t m", t=PACK))
+        nc.vector.tensor_copy(w_sc[:], w_plane[:].rearrange("p (m t) -> p t m", t=PACK))
+
+        def product(acc, lhs, lhs_sc, rhs, rhs_sc, start, stop):
+            nc.tensor.matmul_mx(out=acc, lhsT=lhs, lhsT_scale=lhs_sc, rhs=rhs, rhs_scale=rhs_sc,
+                                start=start, stop=stop)
+
+        xt_op = xt_codes[:].bitcast(E5M2)
+        xo_op = xo_codes[:].bitcast(E4M3)
+        acc_a = [psum.tile([P, J], F32, name="acc_a%d" % t, tag="bank%d" % (2 * t)) for t in range(PACK)]
+        acc_b = [psum.tile([P, J], F32, name="acc_b%d" % t, tag="bank%d" % (2 * t + 1)) for t in range(PACK)]
+        for t in range(PACK):
+            w2_t = w2_codes[:, t, :].bitcast(E5M2)
+            w_t = w_codes[:, t, :].bitcast(U8).bitcast(E2M1)
+            product(acc_a[t][:], w2_t, w2_sc[:, t, :], xo_op, xo_sc[:], True, False)
+            product(acc_b[t][:], w2_t, w2_sc[:, t, :], xt_op, xt_sc[:], True, False)
+            product(acc_a[t][:], w_t, w_sc[:, t, :], xt_op, xt_sc[:], False, True)
+            product(acc_b[t][:], w_t, w_sc[:, t, :], xo_op, xo_sc[:], False, True)
+
+        hid_planes = sb.tile([P, PACK, O], BF16, align_bytes=64)
+        boards = []
+
+        def read_board(t):
+            nc.scalar.activation(hid_planes[:, t, :], boards[t][:].indirect(idx5[:]), COPY)
+
+        pws = [sb.tile([P, C], F32, name="pw%d" % t) for t in range(PACK)]
+        pvs = [sb.tile([P, C], F32, name="pv%d" % t) for t in range(PACK)]
+        for t in range(PACK):
+            nc.vector.memset(pws[t][:], 0.0)
+            nc.vector.memset(pvs[t][:], 0.0)
+
+        def add_boards(t):
+            pg = sb.tile([P, C], F32, name="pg%d" % t)
+            nc.vector.tensor_tensor(pg[:], pws[t][:], pvs[t][:], ADD)
+            boards.append(pg)
+
+        for t in range(PACK):
+            a_sb = sb.tile([P, J], F32, name="a_sb%d" % t)
+            b_sb = sb.tile([P, J], F32, name="b_sb%d" % t)
+            nc.scalar.copy(a_sb[:], acc_a[t][:])
+            nc.vector.tensor_copy(b_sb[:], acc_b[t][:])
+            if t > 0:
+                add_boards(t - 1)
+            nc.scalar.activation(pws[t][:].indirect(idx3[:]), a_sb[:], COPY)
+            nc.vector.tensor_copy(pvs[t][:].indirect(idx4[:]), b_sb[:])
+            if t > 0:
+                read_board(t - 1)
+        add_boards(PACK - 1)
+        read_board(PACK - 1)
+
+        hid = sb.tile([P, O, PACK], BF16, align_bytes=64)
+        nc.vector.tensor_copy(
+            hid[:].rearrange("p (c i) t -> p c t i", i=4),
+            hid_planes[:].rearrange("p t (c i) -> p c t i", i=4),
+        )
+        hid_codes = sb.tile([P, O], U32, align_bytes=64)
+        hid_sc = sb.tile([P, O], U8, align_bytes=64)
+        nc.vector.quantize_mx(out=hid_codes[:].bitcast(E4M3), scales=hid_sc[:],
+                              in_=hid[:].rearrange("p o t -> p (o t)"))
+
+        wb_bytes = wb_raw[:].bitcast(U8)
+        for h in range(N // P):
+            acc_p = psum.tile([P, O], F32, name="acc_p%d" % h, tag="bank%d" % h)
+            product(acc_p[:], wb_bytes[:, 2 * P * h:2 * P * (h + 1)].bitcast(E2M1),
+                    wb_plane[:, P * h:P * (h + 1)], hid_codes[:].bitcast(E4M3), hid_sc[:], True, True)
+            p_sb = sb.tile([P, O], F32, name="p_sb%d" % h)
+            first = sb.tile([P, E], F32, name="first%d" % h)
+            second = sb.tile([P, E], F32, name="second%d" % h)
+            best = sb.tile([P, E], F32, name="best%d" % h)
+            if h == 0:
+                nc.scalar.copy(p_sb[:], acc_p[:])
+                nc.scalar.activation(first[:], p_sb[:].indirect(idx6[:]), COPY)
+                nc.scalar.activation(second[:], p_sb[:].indirect(idx7[:]), COPY)
+            else:
+                nc.vector.tensor_copy(p_sb[:], acc_p[:])
+                nc.vector.tensor_copy(first[:], p_sb[:].indirect(idx6[:]))
+                nc.vector.tensor_copy(second[:], p_sb[:].indirect(idx7[:]))
+            nc.vector.tensor_tensor(best[:], first[:], second[:], MAX)
+            nc.sync.dma_start(out[P * h:P * (h + 1), :], best[:])

@@ -31,48 +31,51 @@ def tile_list_crossed_shared_one_bestoftwo_kernel(
         sb = ctx.enter_context(tc.tile_pool(name="sb", bufs=1))
         psum = ctx.enter_context(tc.psum_pool(name="psum", bufs=1))
 
-        def load_list(src, name):
-            tile = sb.tile(list(src.shape), U16, name=name)
-            nc.sync.dma_start(tile[:], src)
-            return tile
+        def list_tile(src, name):
+            return sb.tile(list(src.shape), U16, name=name)
 
-        def load_words(src, width_bytes, name):
-            tile = sb.tile([P, width_bytes // 4], U32, name=name, align_bytes=64)
-            nc.sync.dma_start(tile[:].bitcast(I32), src.bitcast(I32))
-            return tile
+        def word_tile(width_bytes, name):
+            return sb.tile([P, width_bytes // 4], U32, name=name, align_bytes=64)
 
         def zero_plane(width, name):
             tile = sb.tile([P, width], U8, name=name, align_bytes=64)
-            nc.vector.memset(tile[:].bitcast(I32), 0)
             return tile
 
-        def load_scales(queue, tile, src):
-            for row in range(4):
-                queue.dma_start(tile[row:P:32, :].bitcast(I32), src[0, row:16:4, :].bitcast(I32))
+        def scale_rows(tile, src):
+            return [(tile[32 * q:32 * q + 32, :].bitcast(I32), src[0, 4 * q:4 * q + 4, :].bitcast(I32).partition_broadcast(8)) for q in range(4)]
+
+        def words(tile, src):
+            return (tile[:].bitcast(I32), src.bitcast(I32))
 
         xt_plane = zero_plane(T, "xt_plane")
         xo_plane = zero_plane(Z, "xo_plane")
-        w2_plane = zero_plane(R, "w2_plane")
-        w_plane = zero_plane(R, "w_plane")
+        w_planes = sb.tile([P, 2, R], U8, align_bytes=64)
+        w_plane, w2_plane = w_planes[:, 0, :], w_planes[:, 1, :]
         wb_plane = zero_plane(N, "wb_plane")
+        xt_all, xo_all = word_tile(4 * T, "xt_all"), word_tile(4 * Z, "xo_all")
+        w_raw, w2_raw, wb_raw = word_tile(2 * R, "w_raw"), word_tile(4 * R, "w2_raw"), word_tile(2 * N, "wb_raw")
+        idx, idx2, idx3, idx4 = (list_tile(offs, "idx"), list_tile(offs2, "idx2"),
+                                 list_tile(offs3, "idx3"), list_tile(offs4, "idx4"))
+        idx5, idx6, idx7 = list_tile(offs5, "idx5"), list_tile(offs6, "idx6"), list_tile(offs7, "idx7")
 
-        xt_all = load_words(xt_words[0].rearrange("p n t -> p (n t)"), 4 * T, "xt_all")
-        xo_all = load_words(xo_words[0].rearrange("p n t -> p (n t)"), 4 * Z, "xo_all")
-        idx = load_list(offs, "idx")
-        idx2 = load_list(offs2, "idx2")
-        load_scales(nc.scalar, xt_plane, xt_scales)
-        w2_raw = load_words(w2_words[0].rearrange("p n t -> p (n t)"), 4 * R, "w2_raw")
-        w_raw = load_words(w_words[0], 2 * R, "w_raw")
-        load_scales(nc.scalar, xo_plane, xo_scales)
-        load_scales(nc.scalar, w2_plane, w2_scales)
-        load_scales(nc.scalar, w_plane, w_scales)
-        idx3 = load_list(offs3, "idx3")
-        idx4 = load_list(offs4, "idx4")
-        idx5 = load_list(offs5, "idx5")
-        wb_raw = load_words(wb_words[0], 2 * N, "wb_raw")
-        load_scales(nc.sync, wb_plane, wb_scales)
-        idx6 = load_list(offs6, "idx6")
-        idx7 = load_list(offs7, "idx7")
+        small = [(idx[:], offs), (idx2[:], offs2)]
+        small = small + scale_rows(xt_plane, xt_scales) + scale_rows(xo_plane, xo_scales)
+        small = small + scale_rows(w_plane, w_scales) + scale_rows(w2_plane, w2_scales)
+        large = [
+            words(w_raw, w_words[0]),
+            words(xt_all, xt_words[0].rearrange("p n t -> p (n t)")),
+            words(xo_all, xo_words[0].rearrange("p n t -> p (n t)")),
+            words(w2_raw, w2_words[0].rearrange("p n t -> p (n t)")),
+            (idx3[:], offs3),
+            (idx4[:], offs4),
+        ]
+        loads = []
+        for g in range(3):
+            loads = loads + small[6 * g:6 * g + 6] + large[2 * g:2 * g + 2]
+        loads = loads + [(idx5[:], offs5), words(wb_raw, wb_words[0])] + scale_rows(wb_plane, wb_scales)
+        loads = loads + [(idx6[:], offs6), (idx7[:], offs7)]
+        for dst, src in loads:
+            nc.sync.dma_start(dst, src)
 
         xt_codes = sb.tile([P, J], U32, align_bytes=64)
         xt_sc = sb.tile([P, J], U8, align_bytes=64)
@@ -83,14 +86,17 @@ def tile_list_crossed_shared_one_bestoftwo_kernel(
         nc.vector.tensor_copy(xo_sc[:], xo_plane[:].indirect(idx2[:]))
         nc.vector.tensor_copy(xo_codes[:], xo_all[:].indirect(idx2[:]))
 
-        w2_codes = sb.tile([P, PACK, P], U32, align_bytes=64)
         w_codes = sb.tile([P, PACK, P], U16, align_bytes=64)
-        w2_sc = sb.tile([P, PACK, P], U8, align_bytes=64)
-        w_sc = sb.tile([P, PACK, P], U8, align_bytes=64)
-        nc.scalar.copy(w2_codes[:], w2_raw[:].rearrange("p (m t) -> p t m", t=PACK))
-        nc.vector.tensor_copy(w2_sc[:], w2_plane[:].rearrange("p (m t) -> p t m", t=PACK))
         nc.scalar.copy(w_codes[:], w_raw[:].bitcast(U16).rearrange("p (m t) -> p t m", t=PACK))
-        nc.vector.tensor_copy(w_sc[:], w_plane[:].rearrange("p (m t) -> p t m", t=PACK))
+        w2_codes, w_sc, w2_sc = [], [], []
+        for lo, hi in ((0, 1), (1, PACK)):
+            codes = sb.tile([P, hi - lo, P], U32, name="w2_codes%d" % lo, align_bytes=64)
+            planes = sb.tile([P, 2, hi - lo, P], U8, name="w_scs%d" % lo, align_bytes=64)
+            nc.scalar.copy(codes[:], w2_raw[:].rearrange("p (m t) -> p t m", t=PACK)[:, lo:hi, :])
+            nc.vector.tensor_copy(planes[:], w_planes[:].rearrange("p s (m t) -> p s t m", t=PACK)[:, :, lo:hi, :])
+            w2_codes.extend(codes[:, t, :] for t in range(hi - lo))
+            w_sc.extend(planes[:, 0, t, :] for t in range(hi - lo))
+            w2_sc.extend(planes[:, 1, t, :] for t in range(hi - lo))
 
         def product(acc, lhs, lhs_sc, rhs, rhs_sc, start, stop):
             nc.tensor.matmul_mx(out=acc, lhsT=lhs, lhsT_scale=lhs_sc, rhs=rhs, rhs_scale=rhs_sc,
@@ -101,12 +107,12 @@ def tile_list_crossed_shared_one_bestoftwo_kernel(
         acc_a = [psum.tile([P, J], F32, name="acc_a%d" % t, tag="bank%d" % (2 * t)) for t in range(PACK)]
         acc_b = [psum.tile([P, J], F32, name="acc_b%d" % t, tag="bank%d" % (2 * t + 1)) for t in range(PACK)]
         for t in range(PACK):
-            w2_t = w2_codes[:, t, :].bitcast(E5M2)
+            w2_t = w2_codes[t].bitcast(E5M2)
             w_t = w_codes[:, t, :].bitcast(U8).bitcast(E2M1)
-            product(acc_a[t][:], w2_t, w2_sc[:, t, :], xo_op, xo_sc[:], True, False)
-            product(acc_b[t][:], w2_t, w2_sc[:, t, :], xt_op, xt_sc[:], True, False)
-            product(acc_a[t][:], w_t, w_sc[:, t, :], xt_op, xt_sc[:], False, True)
-            product(acc_b[t][:], w_t, w_sc[:, t, :], xo_op, xo_sc[:], False, True)
+            product(acc_b[t][:], w2_t, w2_sc[t], xt_op, xt_sc[:], True, False)
+            product(acc_b[t][:], w_t, w_sc[t], xo_op, xo_sc[:], False, True)
+            product(acc_a[t][:], w_t, w_sc[t], xt_op, xt_sc[:], True, False)
+            product(acc_a[t][:], w2_t, w2_sc[t], xo_op, xo_sc[:], False, True)
 
         hid_planes = sb.tile([P, PACK, O], BF16, align_bytes=64)
         boards = []
@@ -117,7 +123,7 @@ def tile_list_crossed_shared_one_bestoftwo_kernel(
         pws = [sb.tile([P, C], F32, name="pw%d" % t) for t in range(PACK)]
         pvs = [sb.tile([P, C], F32, name="pv%d" % t) for t in range(PACK)]
         for t in range(PACK):
-            nc.vector.memset(pws[t][:], 0.0)
+            nc.gpsimd.memset(pws[t][:], 0.0)
             nc.vector.memset(pvs[t][:], 0.0)
 
         def add_boards(t):
@@ -125,46 +131,55 @@ def tile_list_crossed_shared_one_bestoftwo_kernel(
             nc.vector.tensor_tensor(pg[:], pws[t][:], pvs[t][:], ADD)
             boards.append(pg)
 
+        a_sb = [sb.tile([P, J], F32, name="a_sb%d" % t) for t in range(PACK)]
+        b_sb = [sb.tile([P, J], F32, name="b_sb%d" % t) for t in range(PACK)]
+
+        def leave_psum(t):
+            nc.scalar.activation(a_sb[t][:], acc_a[t][:], COPY)
+            nc.vector.tensor_copy(b_sb[t][:], acc_b[t][:])
+
+        leave_psum(0)
         for t in range(PACK):
-            a_sb = sb.tile([P, J], F32, name="a_sb%d" % t)
-            b_sb = sb.tile([P, J], F32, name="b_sb%d" % t)
-            nc.scalar.copy(a_sb[:], acc_a[t][:])
-            nc.vector.tensor_copy(b_sb[:], acc_b[t][:])
+            if t + 1 < PACK:
+                leave_psum(t + 1)
             if t > 0:
                 add_boards(t - 1)
-            nc.scalar.activation(pws[t][:].indirect(idx3[:]), a_sb[:], COPY)
-            nc.vector.tensor_copy(pvs[t][:].indirect(idx4[:]), b_sb[:])
+            nc.scalar.activation(pws[t][:].indirect(idx3[:]), a_sb[t][:], COPY)
+            nc.vector.tensor_copy(pvs[t][:].indirect(idx4[:]), b_sb[t][:])
             if t > 0:
                 read_board(t - 1)
         add_boards(PACK - 1)
-        read_board(PACK - 1)
 
-        hid = sb.tile([P, O, PACK], BF16, align_bytes=64)
-        nc.vector.tensor_copy(
-            hid[:].rearrange("p (c i) t -> p c t i", i=4),
-            hid_planes[:].rearrange("p t (c i) -> p c t i", i=4),
-        )
-        hid_codes = sb.tile([P, O], U32, align_bytes=64)
-        hid_sc = sb.tile([P, O], U8, align_bytes=64)
-        nc.vector.quantize_mx(out=hid_codes[:].bitcast(E4M3), scales=hid_sc[:],
-                              in_=hid[:].rearrange("p o t -> p (o t)"))
-
+        H = O // 2
+        last = boards[PACK - 1]
+        nc.vector.tensor_copy(hid_planes[:, PACK - 1, 0:H], last[:].indirect(idx5[:, 0:H // 16]))
+        nc.scalar.activation(hid_planes[:, PACK - 1, H:O], last[:].indirect(idx5[:, H // 16:O // 16]), COPY)
         wb_bytes = wb_raw[:].bitcast(U8)
+        p_sb = [sb.tile([P, O], F32, name="p_sb%d" % h) for h in range(N // P)]
+        for half, move in enumerate((nc.vector.tensor_copy, nc.scalar.copy)):
+            cols = slice(H * half, H * (half + 1))
+            hid = sb.tile([P, H, PACK], BF16, name="hid%d" % half, align_bytes=64)
+            move(hid[:].rearrange("p (c i) t -> p c t i", i=4),
+                 hid_planes[:, :, cols].rearrange("p t (c i) -> p c t i", i=4))
+            hid_codes = sb.tile([P, H], U32, name="hid_codes%d" % half, align_bytes=64)
+            hid_sc = sb.tile([P, H], U8, name="hid_sc%d" % half, align_bytes=64)
+            nc.vector.quantize_mx(out=hid_codes[:].bitcast(E4M3), scales=hid_sc[:],
+                                  in_=hid[:].rearrange("p o t -> p (o t)"))
+            for h, move_out in enumerate((nc.scalar.copy, nc.vector.tensor_copy)):
+                acc_p = psum.tile([P, H], F32, name="acc_p%d%d" % (half, h), tag="bank%d" % (2 * half + h))
+                product(acc_p[:], wb_bytes[:, 2 * P * h:2 * P * (h + 1)].bitcast(E2M1),
+                        wb_plane[:, P * h:P * (h + 1)], hid_codes[:].bitcast(E4M3), hid_sc[:], True, True)
+                move_out(p_sb[h][:, cols], acc_p[:])
+
         for h in range(N // P):
-            acc_p = psum.tile([P, O], F32, name="acc_p%d" % h, tag="bank%d" % h)
-            product(acc_p[:], wb_bytes[:, 2 * P * h:2 * P * (h + 1)].bitcast(E2M1),
-                    wb_plane[:, P * h:P * (h + 1)], hid_codes[:].bitcast(E4M3), hid_sc[:], True, True)
-            p_sb = sb.tile([P, O], F32, name="p_sb%d" % h)
             first = sb.tile([P, E], F32, name="first%d" % h)
             second = sb.tile([P, E], F32, name="second%d" % h)
             best = sb.tile([P, E], F32, name="best%d" % h)
             if h == 0:
-                nc.scalar.copy(p_sb[:], acc_p[:])
-                nc.scalar.activation(first[:], p_sb[:].indirect(idx6[:]), COPY)
-                nc.scalar.activation(second[:], p_sb[:].indirect(idx7[:]), COPY)
+                nc.scalar.activation(first[:], p_sb[h][:].indirect(idx6[:]), COPY)
+                nc.scalar.activation(second[:], p_sb[h][:].indirect(idx7[:]), COPY)
             else:
-                nc.vector.tensor_copy(p_sb[:], acc_p[:])
-                nc.vector.tensor_copy(first[:], p_sb[:].indirect(idx6[:]))
-                nc.vector.tensor_copy(second[:], p_sb[:].indirect(idx7[:]))
+                nc.vector.tensor_copy(first[:], p_sb[h][:].indirect(idx6[:]))
+                nc.vector.tensor_copy(second[:], p_sb[h][:].indirect(idx7[:]))
             nc.vector.tensor_tensor(best[:], first[:], second[:], MAX)
             nc.sync.dma_start(out[P * h:P * (h + 1), :], best[:])

from contextlib import ExitStack

import concourse.mybir as mybir

K, T, Z, J, R, C, O, N, E = 512, 1024, 1024, 256, 512, 512, 256, 256, 128
FLOPS = 2 * (4 * K * R * J + R * N * O)

F32 = mybir.dt.float32
BF16 = mybir.dt.bfloat16
I32 = mybir.dt.int32
U32 = mybir.dt.uint32
U16 = mybir.dt.uint16
U8 = mybir.dt.uint8
E4M3 = mybir.dt.float8_e4m3fn_x4
E5M2 = mybir.dt.float8_e5m2_x4
E2M1 = mybir.dt.float4_e2m1fn_x4
COPY = mybir.ActivationFunctionType.Copy
ADD = mybir.AluOpType.add
MAX = mybir.AluOpType.max

P = 128
PACK = 4


def tile_list_crossed_shared_one_bestoftwo_kernel(
    tc, xt_words, xt_scales, xo_words, xo_scales, w_words, w_scales, w2_words, w2_scales,
    wb_words, wb_scales, offs, offs2, offs3, offs4, offs5, offs6, offs7, out,
):
    nc = tc.nc
    with ExitStack() as ctx:
        sb = ctx.enter_context(tc.tile_pool(name="sb", bufs=1))
        psum = ctx.enter_context(tc.psum_pool(name="psum", bufs=1))

        def list_tile(src, name):
            return sb.tile(list(src.shape), U16, name=name)

        def word_tile(width_bytes, name):
            return sb.tile([P, width_bytes // 4], U32, name=name, align_bytes=64)

        def zero_plane(width, name):
            tile = sb.tile([P, width], U8, name=name, align_bytes=64)
            return tile

        def scale_rows(tile, src):
            return [(tile[32 * q:32 * q + 32, :].bitcast(I32), src[0, 4 * q:4 * q + 4, :].bitcast(I32).partition_broadcast(8)) for q in range(4)]

        def words(tile, src):
            return (tile[:].bitcast(I32), src.bitcast(I32))

        xt_plane = zero_plane(T, "xt_plane")
        xo_plane = zero_plane(Z, "xo_plane")
        w_planes = sb.tile([P, 2, R], U8, align_bytes=64)
        w_plane, w2_plane = w_planes[:, 0, :], w_planes[:, 1, :]
        wb_plane = zero_plane(N, "wb_plane")
        xt_all, xo_all = word_tile(4 * T, "xt_all"), word_tile(4 * Z, "xo_all")
        w_raw, w2_raw, wb_raw = word_tile(2 * R, "w_raw"), word_tile(4 * R, "w2_raw"), word_tile(2 * N, "wb_raw")
        idx, idx2, idx3, idx4 = (list_tile(offs, "idx"), list_tile(offs2, "idx2"),
                                 list_tile(offs3, "idx3"), list_tile(offs4, "idx4"))
        idx5, idx6, idx7 = list_tile(offs5, "idx5"), list_tile(offs6, "idx6"), list_tile(offs7, "idx7")

        small = [(idx[:], offs), (idx2[:], offs2)]
        small = small + scale_rows(xt_plane, xt_scales) + scale_rows(xo_plane, xo_scales)
        small = small + scale_rows(w_plane, w_scales) + scale_rows(w2_plane, w2_scales)
        large = [
            words(w_raw, w_words[0]),
            words(xt_all, xt_words[0].rearrange("p n t -> p (n t)")),
            words(xo_all, xo_words[0].rearrange("p n t -> p (n t)")),
            words(w2_raw, w2_words[0].rearrange("p n t -> p (n t)")),
            (idx3[:], offs3),
            (idx4[:], offs4),
        ]
        loads = []
        for g in range(3):
            loads = loads + small[6 * g:6 * g + 6] + large[2 * g:2 * g + 2]
        loads = loads + [(idx5[:], offs5), words(wb_raw, wb_words[0])] + scale_rows(wb_plane, wb_scales)
        loads = loads + [(idx6[:], offs6), (idx7[:], offs7)]
        for dst, src in loads:
            nc.sync.dma_start(dst, src)

        xt_codes = sb.tile([P, J], U32, align_bytes=64)
        xt_sc = sb.tile([P, J], U8, align_bytes=64)
        xo_codes = sb.tile([P, J], U32, align_bytes=64)
        xo_sc = sb.tile([P, J], U8, align_bytes=64)
        nc.vector.tensor_copy(xt_sc[:], xt_plane[:].indirect(idx[:]))
        nc.vector.tensor_copy(xt_codes[:], xt_all[:].indirect(idx[:]))
        nc.vector.tensor_copy(xo_sc[:], xo_plane[:].indirect(idx2[:]))
        nc.vector.tensor_copy(xo_codes[:], xo_all[:].indirect(idx2[:]))

        w_codes = sb.tile([P, PACK, P], U16, align_bytes=64)
        nc.scalar.copy(w_codes[:], w_raw[:].bitcast(U16).rearrange("p (m t) -> p t m", t=PACK))
        w2_codes, w_sc, w2_sc = [], [], []
        for lo, hi in ((0, 1), (1, PACK)):
            codes = sb.tile([P, hi - lo, P], U32, name="w2_codes%d" % lo, align_bytes=64)
            planes = sb.tile([P, 2, hi - lo, P], U8, name="w_scs%d" % lo, align_bytes=64)
            nc.scalar.copy(codes[:], w2_raw[:].rearrange("p (m t) -> p t m", t=PACK)[:, lo:hi, :])
            nc.vector.tensor_copy(planes[:], w_planes[:].rearrange("p s (m t) -> p s t m", t=PACK)[:, :, lo:hi, :])
            w2_codes.extend(codes[:, t, :] for t in range(hi - lo))
            w_sc.extend(planes[:, 0, t, :] for t in range(hi - lo))
            w2_sc.extend(planes[:, 1, t, :] for t in range(hi - lo))

        def product(acc, lhs, lhs_sc, rhs, rhs_sc, start, stop):
            nc.tensor.matmul_mx(out=acc, lhsT=lhs, lhsT_scale=lhs_sc, rhs=rhs, rhs_scale=rhs_sc,
                                start=start, stop=stop)

        xt_op = xt_codes[:].bitcast(E5M2)
        xo_op = xo_codes[:].bitcast(E4M3)
        acc_a = [psum.tile([P, J], F32, name="acc_a%d" % t, tag="bank%d" % (2 * t)) for t in range(PACK)]
        acc_b = [psum.tile([P, J], F32, name="acc_b%d" % t, tag="bank%d" % (2 * t + 1)) for t in range(PACK)]
        for t in range(PACK):
            w2_t = w2_codes[t].bitcast(E5M2)
            w_t = w_codes[:, t, :].bitcast(U8).bitcast(E2M1)
            product(acc_b[t][:], w2_t, w2_sc[t], xt_op, xt_sc[:], True, False)
            product(acc_b[t][:], w_t, w_sc[t], xo_op, xo_sc[:], False, True)
            product(acc_a[t][:], w_t, w_sc[t], xt_op, xt_sc[:], True, False)
            product(acc_a[t][:], w2_t, w2_sc[t], xo_op, xo_sc[:], False, True)

        hid_planes = sb.tile([P, PACK, O], BF16, align_bytes=64)
        boards = []

        def read_board(t):
            nc.scalar.activation(hid_planes[:, t, :], boards[t][:].indirect(idx5[:]), COPY)

        pws = [sb.tile([P, C], F32, name="pw%d" % t) for t in range(PACK)]
        pvs = [sb.tile([P, C], F32, name="pv%d" % t) for t in range(PACK)]
        for t in range(PACK):
            nc.gpsimd.memset(pws[t][:], 0.0)
            nc.vector.memset(pvs[t][:], 0.0)

        def add_boards(t):
            pg = sb.tile([P, C], F32, name="pg%d" % t)
            nc.vector.tensor_tensor(pg[:], pws[t][:], pvs[t][:], ADD)
            boards.append(pg)

        a_sb = [sb.tile([P, J], F32, name="a_sb%d" % t) for t in range(PACK)]
        b_sb = [sb.tile([P, J], F32, name="b_sb%d" % t) for t in range(PACK)]

        def leave_psum(t):
            nc.scalar.activation(a_sb[t][:], acc_a[t][:], COPY)
            nc.vector.tensor_copy(b_sb[t][:], acc_b[t][:])

        leave_psum(0)
        for t in range(PACK):
            if t + 1 < PACK:
                leave_psum(t + 1)
            if t > 0:
                add_boards(t - 1)
            nc.scalar.activation(pws[t][:].indirect(idx3[:]), a_sb[t][:], COPY)
            nc.vector.tensor_copy(pvs[t][:].indirect(idx4[:]), b_sb[t][:])
            if t > 0:
                read_board(t - 1)
        add_boards(PACK - 1)

        H = O // 2
        last = boards[PACK - 1]
        nc.vector.tensor_copy(hid_planes[:, PACK - 1, 0:H], last[:].indirect(idx5[:, 0:H // 16]))
        nc.scalar.activation(hid_planes[:, PACK - 1, H:O], last[:].indirect(idx5[:, H // 16:O // 16]), COPY)
        wb_bytes = wb_raw[:].bitcast(U8)
        p_sb = [sb.tile([P, O], F32, name="p_sb%d" % h) for h in range(N // P)]
        for half, move in enumerate((nc.vector.tensor_copy, nc.scalar.copy)):
            cols = slice(H * half, H * (half + 1))
            hid = sb.tile([P, H, PACK], BF16, name="hid%d" % half, align_bytes=64)
            move(hid[:].rearrange("p (c i) t -> p c t i", i=4),
                 hid_planes[:, :, cols].rearrange("p t (c i) -> p c t i", i=4))
            hid_codes = sb.tile([P, H], U32, name="hid_codes%d" % half, align_bytes=64)
            hid_sc = sb.tile([P, H], U8, name="hid_sc%d" % half, align_bytes=64)
            nc.vector.quantize_mx(out=hid_codes[:].bitcast(E4M3), scales=hid_sc[:],
                                  in_=hid[:].rearrange("p o t -> p (o t)"))
            for h, move_out in enumerate((nc.scalar.copy, nc.vector.tensor_copy)):
                acc_p = psum.tile([P, H], F32, name="acc_p%d%d" % (half, h), tag="bank%d" % (2 * half + h))
                product(acc_p[:], wb_bytes[:, 2 * P * h:2 * P * (h + 1)].bitcast(E2M1),
                        wb_plane[:, P * h:P * (h + 1)], hid_codes[:].bitcast(E4M3), hid_sc[:], True, True)
                move_out(p_sb[h][:, cols], acc_p[:])

        for h in range(N // P):
            first = sb.tile([P, E], F32, name="first%d" % h)
            second = sb.tile([P, E], F32, name="second%d" % h)
            best = sb.tile([P, E], F32, name="best%d" % h)
            if h == 0:
                nc.scalar.activation(first[:], p_sb[h][:].indirect(idx6[:]), COPY)
                nc.scalar.activation(second[:], p_sb[h][:].indirect(idx7[:]), COPY)
            else:
                nc.vector.tensor_copy(first[:], p_sb[h][:].indirect(idx6[:]))
                nc.vector.tensor_copy(second[:], p_sb[h][:].indirect(idx7[:]))
            nc.vector.tensor_tensor(best[:], first[:], second[:], MAX)
            nc.sync.dma_start(out[P * h:P * (h + 1), :], best[:])
